import numpy as np
import ml_dtypes


def mxq(x, axis, fmt="e4m3"):
    dtype, down = {"e4m3": (ml_dtypes.float8_e4m3fn, 7), "e5m2": (ml_dtypes.float8_e5m2, 14)}[fmt]
    v = np.moveaxis(np.asarray(x, np.float32).astype(ml_dtypes.bfloat16).astype(np.float64), axis, -1)
    blocks = v.reshape(v.shape[:-1] + (-1, 32))
    amax = np.abs(blocks).max(-1, keepdims=True)
    byte = np.maximum(np.where(amax > 0, np.frexp(amax)[1] - 1 + 127, 0) - down, 1)
    scale = np.exp2(byte - 127.0)
    codes = (blocks / scale).astype(np.float32).astype(dtype).astype(np.float64)
    return np.moveaxis((codes * scale).reshape(v.shape), -1, axis)


WIDE = False


def mx_kscale(k):
    if not WIDE:
        return np.ones(k)
    levels = np.array([10, -10, 5, -5, 0])
    if k % 512:
        return np.exp2(np.random.permutation(np.resize(levels, k // 32))).repeat(32)
    a = np.empty((k // 512, 16))
    for p in range(k // 512):
        a[p, :8] = np.random.permutation(np.resize(levels, 8))
        for g in range(8):
            far = levels[np.abs(levels - a[p, g]) >= 10]
            a[p, g + 8] = far[np.random.randint(len(far))]
    return np.exp2(a.ravel()).repeat(32)


def f64(x):
    return np.asarray(x).astype(np.float64)


def striped(idx):
    return np.tile(np.asarray(idx).reshape(-1, 16).T, (8, 1)).astype(np.uint16)


def unstriped(offs):
    return offs[:16].T.reshape(-1).astype(np.int64)


def sigmoid(v):
    return 1.0 / (1.0 + np.exp(-v))


D, T, I, Q, E, U, X = 512, 2048, 512, 128, 512, 1024, 1024


def setup_inputs():
    n = np.random.standard_normal
    idx = np.random.permutation(T)[:I]
    idx2 = np.random.permutation(U)[:I]
    idx3 = np.random.permutation(X)[:I]
    fd = mx_kscale(D)
    fi = mx_kscale(I)
    ti = np.ones(T)
    ti[idx] = fi
    ti3 = np.ones(X)
    ti3[idx3] = fi
    return {
        "query": (n((D, Q)) * 0.9 / np.sqrt(D) * fd[:, None]).astype(np.float32),
        "keys": (n((D, T)) / fd[:, None]).astype(np.float32),
        "notes": (n((D, U)) / fd[:, None]).astype(np.float32),
        "os": (np.random.uniform(0.02, 0.08, (1, I)) * fi).astype(np.float32),
        "os2": (np.random.uniform(0.02, 0.08, (1, I)) * fi).astype(np.float32),
        "vals": (n((E, T)) / ti).astype(np.float32),
        "vals2": (n((E, X)) / ti3).astype(np.float32),
        "offs": striped(idx),
        "offs2": striped(idx2),
        "offs3": striped(idx3),
    }


def reference(query, keys, notes, os, os2, vals, vals2, offs, offs2, offs3):
    idx = unstriped(offs)
    idx2 = unstriped(offs2)
    idx3 = unstriped(offs3)
    zk = np.maximum(f64(keys)[:, idx], f64(notes)[:, idx2])
    queryq = mxq(f64(query), 0, "e4m3")
    zkq = mxq(zk, 0, "e4m3")
    s = queryq.T @ zkq
    w = sigmoid(s)
    wo1 = w * f64(os)
    wt1 = wo1.T
    wo2 = w * f64(os2)
    wt2 = wo2.T
    vt1 = f64(vals)[:, idx].T
    vt2 = f64(vals2)[:, idx3].T
    wt1q = mxq(wt1, 0, "e4m3")
    vt1q = mxq(vt1, 0, "e4m3")
    wt2q = mxq(wt2, 0, "e4m3")
    vt2q = mxq(vt2, 0, "e4m3")
    o = wt1q.T @ vt1q + wt2q.T @ vt2q
    return o

@@ -1,0 +1,177 @@
+from contextlib import ExitStack
+
+import concourse.mybir as mybir
+from concourse.masks import make_identity
+
+D, T, I, Q, E, U, X = 512, 2048, 512, 128, 512, 1024, 1024
+FLOPS = 2 * Q * I * D + 2 * 2 * Q * I * E
+
+F32 = mybir.dt.float32
+BF16 = mybir.dt.bfloat16
+U32 = mybir.dt.uint32
+U16 = mybir.dt.uint16
+U8 = mybir.dt.uint8
+FP8X4 = mybir.dt.float8_e4m3fn_x4
+ALU = mybir.AluOpType
+ACT = mybir.ActivationFunctionType
+
+P = 128
+PACK = 4
+BLOCKS = E // P
+LIST_COLS = I // 16
+
+
+def tile_attend_keylarger_twostores_lean_kernel(
+    tc, query, keys, notes, factor1, factor2, vals, vals2, offs, offs2, offs3, out
+):
+    nc = tc.nc
+    with ExitStack() as ctx:
+        keep = ctx.enter_context(tc.tile_pool(name="keep", bufs=1))
+        ring = ctx.enter_context(tc.tile_pool(name="ring", bufs=4))
+        psum = ctx.enter_context(tc.psum_pool(name="psum", bufs=1))
+        turn = ctx.enter_context(tc.psum_pool(name="turn", bufs=4))
+
+        list1 = keep.tile([P, LIST_COLS], U16, name="list1")
+        list2 = keep.tile([P, LIST_COLS], U16, name="list2")
+        list3 = keep.tile([P, LIST_COLS], U16, name="list3")
+        key_pool = [keep.tile([P, T], F32, name=f"key_pool{j}") for j in range(PACK)]
+        note_pool = [keep.tile([P, U], F32, name=f"note_pool{j}") for j in range(PACK)]
+        val1_pool = [keep.tile([P, T], F32, name=f"val1_pool{b}") for b in range(BLOCKS)]
+        val2_pool = [keep.tile([P, X], F32, name=f"val2_pool{b}") for b in range(BLOCKS)]
+        query_raw = keep.tile([P, PACK, Q], F32, name="query_raw")
+        factor1_col = keep.tile([P, PACK], F32, name="factor1_col")
+        factor2_col = keep.tile([P, PACK], F32, name="factor2_col")
+
+        key_rows = keys.rearrange("(p j) t -> p j t", j=PACK)
+        note_rows = notes.rearrange("(p j) u -> p j u", j=PACK)
+        for j in range(PACK):
+            nc.sync.dma_start(out=key_pool[j][:], in_=key_rows[:, j, :])
+            if j == 0:
+                nc.sync.dma_start(list1[:], offs)
+                nc.sync.dma_start(list2[:], offs2)
+            nc.sync.dma_start(out=note_pool[j][:], in_=note_rows[:, j, :])
+        nc.sync.dma_start(out=query_raw[:], in_=query.rearrange("(p j) q -> p j q", j=PACK))
+        nc.sync.dma_start(list3[:], offs3)
+        nc.sync.dma_start(out=factor1_col[:], in_=factor1.rearrange("o (p t) -> (o p) t", t=PACK))
+        nc.sync.dma_start(out=factor2_col[:], in_=factor2.rearrange("o (p t) -> (o p) t", t=PACK))
+        for b in range(BLOCKS):
+            nc.sync.dma_start(out=val2_pool[b][:], in_=vals2[b * P : (b + 1) * P, :])
+            nc.sync.dma_start(out=val1_pool[b][:], in_=vals[b * P : (b + 1) * P, :])
+
+        identity = keep.tile([P, P], F32, name="identity")
+        make_identity(nc, identity[:])
+
+        key_listed = keep.tile([P, PACK, I], F32, name="key_listed")
+        note_listed = keep.tile([P, PACK, I], F32, name="note_listed")
+        for j in range(PACK):
+            nc.scalar.activation(key_listed[:, j, :], key_pool[j][:].indirect(list1[:]), ACT.Copy)
+            nc.vector.tensor_copy(note_listed[:, j, :], note_pool[j][:].indirect(list2[:]))
+
+        zk = keep.tile([P, PACK, P, PACK], BF16, name="zk", align_bytes=64)
+        nc.vector.tensor_tensor(
+            out=zk[:].rearrange("p t s j -> p s j t"),
+            in0=key_listed[:].rearrange("p j (s t) -> p s j t", t=PACK),
+            in1=note_listed[:].rearrange("p j (s t) -> p s j t", t=PACK),
+            op=ALU.max,
+        )
+        query_words = keep.tile([P, Q, PACK], BF16, name="query_words", align_bytes=64)
+        nc.scalar.copy(out=query_words[:], in_=query_raw[:].rearrange("p j q -> p q j"))
+
+        zk_codes = keep.tile([P, I], U32, name="zk_codes", align_bytes=64)
+        zk_scales = keep.tile([P, I], U8, name="zk_scales", align_bytes=64)
+        query_codes = keep.tile([P, Q], U32, name="query_codes", align_bytes=64)
+        query_scales = keep.tile([P, Q], U8, name="query_scales", align_bytes=64)
+        nc.vector.quantize_mx(
+            out=query_codes[:].bitcast(FP8X4),
+            scales=query_scales[:],
+            in_=query_words[:].rearrange("p q j -> p (q j)"),
+        )
+        nc.vector.quantize_mx(
+            out=zk_codes[:].bitcast(FP8X4),
+            scales=zk_scales[:],
+            in_=zk[:].rearrange("p t s j -> p (t s j)"),
+        )
+
+        scores = psum.tile([P, PACK, Q], F32, name="scores")
+        for t in range(PACK):
+            cols = slice(t * P, (t + 1) * P)
+            nc.tensor.matmul_mx(
+                out=scores[:, t, :],
+                lhsT=zk_codes[:, cols].bitcast(FP8X4),
+                lhsT_scale=zk_scales[:, cols],
+                rhs=query_codes[:].bitcast(FP8X4),
+                rhs_scale=query_scales[:],
+                start=True,
+                stop=True,
+            )
+        weights = keep.tile([P, Q, PACK], F32, name="weights")
+        nc.scalar.activation(weights[:], scores[:].rearrange("p t q -> p q t"), ACT.Sigmoid)
+
+        wt = keep.tile([P, 2, Q, PACK], BF16, name="wt", align_bytes=64)
+        for store, factor_col in enumerate((factor1_col, factor2_col)):
+            nc.vector.tensor_tensor(
+                out=wt[:, store, :, :],
+                in0=weights[:],
+                in1=factor_col[:].unsqueeze(1).to_broadcast([P, Q, PACK]),
+                op=ALU.mult,
+            )
+        wt_codes = keep.tile([P, 2 * Q], U32, name="wt_codes", align_bytes=64)
+        wt_scales = keep.tile([P, 2 * Q], U8, name="wt_scales", align_bytes=64)
+        nc.vector.quantize_mx(
+            out=wt_codes[:].bitcast(FP8X4),
+            scales=wt_scales[:],
+            in_=wt[:].rearrange("p n q t -> p (n q t)"),
+        )
+
+        vt_codes = [keep.tile([P, E], U32, name=f"vt_codes{n}", align_bytes=64) for n in range(2)]
+        vt_scales = [keep.tile([P, E], U8, name=f"vt_scales{n}", align_bytes=64) for n in range(2)]
+
+        def turn_and_quantise(listed, store, b):
+            pairs = listed[:].bitcast(F32)
+            turned = turn.tile([P, 2, P], F32, name="turned")
+            for u in range(2):
+                nc.tensor.transpose(turned[:, u, :], pairs[:, u : I // 2 : 2], identity[:])
+            vt = ring.tile([P, P, 2], F32, name="vt", align_bytes=64)
+            nc.scalar.copy(out=vt[:], in_=turned[:].rearrange("p u e -> p e u"))
+            cols = slice(b * P, (b + 1) * P)
+            nc.vector.quantize_mx(
+                out=vt_codes[store][:, cols].bitcast(FP8X4),
+                scales=vt_scales[store][:, cols],
+                in_=vt[:].rearrange("p e u -> p (e u)").bitcast(BF16),
+            )
+
+        def multiply_and_store(first, last):
+            cols = slice(first * P, last * P)
+            width = (last - first) * P
+            acc = psum.tile([P, width], F32, name=f"acc{first}")
+            for store in (1, 0):
+                rows = slice(store * Q, (store + 1) * Q)
+                nc.tensor.matmul_mx(
+                    out=acc[:],
+                    lhsT=wt_codes[:, rows].bitcast(FP8X4),
+                    lhsT_scale=wt_scales[:, rows],
+                    rhs=vt_codes[store][:, cols].bitcast(FP8X4),
+                    rhs_scale=vt_scales[store][:, cols],
+                    start=(store == 1),
+                    stop=(store == 0),
+                )
+            result = keep.tile([P, width], F32, name=f"result{first}")
+            nc.vector.tensor_copy(out=result[:], in_=acc[:])
+            nc.sync.dma_start(out=out[:, cols], in_=result[:])
+
+        for b in range(BLOCKS):
+            listed2 = ring.tile([P, I], BF16, name="listed2")
+            nc.vector.tensor_copy(listed2[:], val2_pool[b][:].indirect(list3[:]))
+            turn_and_quantise(listed2, 1, b)
+            listed1 = ring.tile([P, I], BF16, name="listed1")
+            if b < BLOCKS - 1:
+                nc.scalar.activation(listed1[:], val1_pool[b][:].indirect(list1[:]), ACT.Copy)
+            else:
+                half = LIST_COLS // 2
+                nc.vector.tensor_copy(listed1[:, : I // 2], val1_pool[b][:].indirect(list1[:, :half]))
+                nc.scalar.activation(listed1[:, I // 2 :], val1_pool[b][:].indirect(list1[:, half:]), ACT.Copy)
+            turn_and_quantise(listed1, 0, b)
+            if b == 1:
+                multiply_and_store(0, 2)
+            elif b > 1:
+                multiply_and_store(b, b + 1)

@@ -18,7 +18,10 @@ ACT = mybir.ActivationFunctionType
 P = 128
 PACK = 4
 BLOCKS = E // P
-LIST_COLS = I // 16
+SLOTS_PER_COLUMN = 16
+FIRST, SECOND = 0, 1
+VECTOR_SHARE = 288
+ALIGN = 64
 
 
 def tile_attend_keylarger_twostores_lean_kernel(
@@ -27,151 +30,178 @@ def tile_attend_keylarger_twostores_lean_kernel(
     nc = tc.nc
     with ExitStack() as ctx:
         keep = ctx.enter_context(tc.tile_pool(name="keep", bufs=1))
-        ring = ctx.enter_context(tc.tile_pool(name="ring", bufs=4))
         psum = ctx.enter_context(tc.psum_pool(name="psum", bufs=1))
         turn = ctx.enter_context(tc.psum_pool(name="turn", bufs=4))
 
-        list1 = keep.tile([P, LIST_COLS], U16, name="list1")
-        list2 = keep.tile([P, LIST_COLS], U16, name="list2")
-        list3 = keep.tile([P, LIST_COLS], U16, name="list3")
-        key_pool = [keep.tile([P, T], F32, name=f"key_pool{j}") for j in range(PACK)]
-        note_pool = [keep.tile([P, U], F32, name=f"note_pool{j}") for j in range(PACK)]
-        val1_pool = [keep.tile([P, T], F32, name=f"val1_pool{b}") for b in range(BLOCKS)]
-        val2_pool = [keep.tile([P, X], F32, name=f"val2_pool{b}") for b in range(BLOCKS)]
-        query_raw = keep.tile([P, PACK, Q], F32, name="query_raw")
-        factor1_col = keep.tile([P, PACK], F32, name="factor1_col")
-        factor2_col = keep.tile([P, PACK], F32, name="factor2_col")
+        def sbuf(name, shape, dtype, buffer=None):
+            return keep.tile(shape, dtype, name=name, tag=buffer or name, align_bytes=ALIGN)[:]
 
-        key_rows = keys.rearrange("(p j) t -> p j t", j=PACK)
-        note_rows = notes.rearrange("(p j) u -> p j u", j=PACK)
-        for j in range(PACK):
-            nc.sync.dma_start(out=key_pool[j][:], in_=key_rows[:, j, :])
-            if j == 0:
-                nc.sync.dma_start(list1[:], offs)
-                nc.sync.dma_start(list2[:], offs2)
-            nc.sync.dma_start(out=note_pool[j][:], in_=note_rows[:, j, :])
-        nc.sync.dma_start(out=query_raw[:], in_=query.rearrange("(p j) q -> p j q", j=PACK))
-        nc.sync.dma_start(list3[:], offs3)
-        nc.sync.dma_start(out=factor1_col[:], in_=factor1.rearrange("o (p t) -> (o p) t", t=PACK))
-        nc.sync.dma_start(out=factor2_col[:], in_=factor2.rearrange("o (p t) -> (o p) t", t=PACK))
+        token_list = sbuf("token_list", [P, I // SLOTS_PER_COLUMN], U16)
+        note_list = sbuf("note_list", [P, I // SLOTS_PER_COLUMN], U16)
+        column_list = sbuf("column_list", [P, I // SLOTS_PER_COLUMN], U16)
+        key_planes01 = sbuf("key_planes01", [P, 2 * T], F32)
+        key_plane2 = sbuf("key_plane2", [P, T], F32)
+        key_plane3 = sbuf("key_plane3", [P, T], F32)
+        key_planes = [key_planes01[:, :T], key_planes01[:, T:], key_plane2, key_plane3]
+        note_pairs = [sbuf(f"note_pair{h}", [P, 2 * U], F32) for h in range(2)]
+        note_planes = [note_pairs[j // 2][:, (j % 2) * U : (j % 2 + 1) * U] for j in range(PACK)]
+        first_store = [sbuf(f"first_store{b}", [P, T], F32) for b in range(BLOCKS)]
+        second_store = [sbuf(f"second_store{b}", [P, X], F32) for b in range(BLOCKS)]
+        query_rows = sbuf("query_rows", [P, PACK, Q], F32)
+        factors = [sbuf(f"factor{store}", [P, PACK], F32) for store in (FIRST, SECOND)]
+
+        key_rows = keys.rearrange("(p j) t -> p (j t)", j=PACK)
+        note_rows = notes.rearrange("(p j) u -> p (j u)", j=PACK)
+        nc.sync.dma_start(out=second_store[0], in_=vals2[:P, :])
+        nc.sync.dma_start(column_list, offs3)
+        nc.sync.dma_start(out=note_pairs[0], in_=note_rows[:, : 2 * U])
+        nc.sync.dma_start(note_list, offs2)
+        for b in range(1, BLOCKS):
+            nc.scalar.dma_start(out=second_store[b], in_=vals2[b * P : (b + 1) * P, :])
+        nc.sync.dma_start(out=key_planes01, in_=key_rows[:, : 2 * T])
+        nc.sync.dma_start(token_list, offs)
+        nc.sync.dma_start(out=note_pairs[1], in_=note_rows[:, 2 * U :])
+        nc.sync.dma_start(out=key_plane2, in_=key_rows[:, 2 * T : 3 * T])
+        nc.sync.dma_start(out=key_plane3, in_=key_rows[:, 3 * T :])
+        nc.sync.dma_start(out=query_rows, in_=query.rearrange("(p j) q -> p j q", j=PACK))
         for b in range(BLOCKS):
-            nc.sync.dma_start(out=val2_pool[b][:], in_=vals2[b * P : (b + 1) * P, :])
-            nc.sync.dma_start(out=val1_pool[b][:], in_=vals[b * P : (b + 1) * P, :])
+            nc.sync.dma_start(out=first_store[b], in_=vals[b * P : (b + 1) * P, :])
+        for factor, row in zip(factors, (factor1, factor2)):
+            nc.gpsimd.dma_start(out=factor, in_=row.rearrange("o (p t) -> (o p) t", t=PACK))
 
-        identity = keep.tile([P, P], F32, name="identity")
-        make_identity(nc, identity[:])
+        identity = sbuf("identity", [P, P], F32)
+        make_identity(nc, identity)
 
-        key_listed = keep.tile([P, PACK, I], F32, name="key_listed")
-        note_listed = keep.tile([P, PACK, I], F32, name="note_listed")
-        for j in range(PACK):
-            nc.scalar.activation(key_listed[:, j, :], key_pool[j][:].indirect(list1[:]), ACT.Copy)
-            nc.vector.tensor_copy(note_listed[:, j, :], note_pool[j][:].indirect(list2[:]))
+        def gather(listed, window, offsets, on_vector):
+            cut = on_vector // SLOTS_PER_COLUMN
+            if on_vector > 0:
+                nc.vector.tensor_copy(listed[:, :on_vector], window.indirect(offsets[:, :cut]))
+            if on_vector < I:
+                nc.scalar.activation(listed[:, on_vector:], window.indirect(offsets[:, cut:]), ACT.Copy)
 
-        zk = keep.tile([P, PACK, P, PACK], BF16, name="zk", align_bytes=64)
-        nc.vector.tensor_tensor(
-            out=zk[:].rearrange("p t s j -> p s j t"),
-            in0=key_listed[:].rearrange("p j (s t) -> p s j t", t=PACK),
-            in1=note_listed[:].rearrange("p j (s t) -> p s j t", t=PACK),
-            op=ALU.max,
-        )
-        query_words = keep.tile([P, Q, PACK], BF16, name="query_words", align_bytes=64)
-        nc.scalar.copy(out=query_words[:], in_=query_raw[:].rearrange("p j q -> p q j"))
+        def quantise(name, words):
+            columns = words.shape[1] // PACK
+            codes = sbuf(f"{name}_codes", [P, columns], U32)
+            scales = sbuf(f"{name}_scales", [P, columns], U8)
+            nc.vector.quantize_mx(out=codes.bitcast(FP8X4), scales=scales, in_=words)
+            return codes, scales
 
-        zk_codes = keep.tile([P, I], U32, name="zk_codes", align_bytes=64)
-        zk_scales = keep.tile([P, I], U8, name="zk_scales", align_bytes=64)
-        query_codes = keep.tile([P, Q], U32, name="query_codes", align_bytes=64)
-        query_scales = keep.tile([P, Q], U8, name="query_scales", align_bytes=64)
-        nc.vector.quantize_mx(
-            out=query_codes[:].bitcast(FP8X4),
-            scales=query_scales[:],
-            in_=query_words[:].rearrange("p q j -> p (q j)"),
-        )
-        nc.vector.quantize_mx(
-            out=zk_codes[:].bitcast(FP8X4),
-            scales=zk_scales[:],
-            in_=zk[:].rearrange("p t s j -> p (t s j)"),
-        )
+        def columns_of(quantised, n):
+            return [part[:, n * P : (n + 1) * P] for part in quantised]
 
-        scores = psum.tile([P, PACK, Q], F32, name="scores")
-        for t in range(PACK):
-            cols = slice(t * P, (t + 1) * P)
+        def multiply(acc, stationary, moving, start, stop):
             nc.tensor.matmul_mx(
-                out=scores[:, t, :],
-                lhsT=zk_codes[:, cols].bitcast(FP8X4),
-                lhsT_scale=zk_scales[:, cols],
-                rhs=query_codes[:].bitcast(FP8X4),
-                rhs_scale=query_scales[:],
-                start=True,
-                stop=True,
+                out=acc,
+                lhsT=stationary[0].bitcast(FP8X4),
+                lhsT_scale=stationary[1],
+                rhs=moving[0].bitcast(FP8X4),
+                rhs_scale=moving[1],
+                start=start,
+                stop=stop,
             )
-        weights = keep.tile([P, Q, PACK], F32, name="weights")
-        nc.scalar.activation(weights[:], scores[:].rearrange("p t q -> p q t"), ACT.Sigmoid)
 
-        wt = keep.tile([P, 2, Q, PACK], BF16, name="wt", align_bytes=64)
-        for store, factor_col in enumerate((factor1_col, factor2_col)):
+        keys_listed = [sbuf(f"keys_listed{h}", [P, 2, I], F32) for h in range(2)]
+        notes_listed = [sbuf(f"notes_listed{h}", [P, 2, I], F32) for h in range(2)]
+        zk_pairs = sbuf("zk_pairs", [P, 2, I, 2], BF16)
+
+        def gather_keys(j, on_vector):
+            gather(keys_listed[j // 2][:, j % 2, :], key_planes[j], token_list, on_vector)
+
+        def gather_notes(j, on_vector):
+            gather(notes_listed[j // 2][:, j % 2, :], note_planes[j], note_list, on_vector)
+
+        def larger(h):
             nc.vector.tensor_tensor(
-                out=wt[:, store, :, :],
-                in0=weights[:],
-                in1=factor_col[:].unsqueeze(1).to_broadcast([P, Q, PACK]),
-                op=ALU.mult,
+                out=zk_pairs[:, h],
+                in0=keys_listed[h].rearrange("p j i -> p i j"),
+                in1=notes_listed[h].rearrange("p j i -> p i j"),
+                op=ALU.max,
             )
-        wt_codes = keep.tile([P, 2 * Q], U32, name="wt_codes", align_bytes=64)
-        wt_scales = keep.tile([P, 2 * Q], U8, name="wt_scales", align_bytes=64)
-        nc.vector.quantize_mx(
-            out=wt_codes[:].bitcast(FP8X4),
-            scales=wt_scales[:],
-            in_=wt[:].rearrange("p n q t -> p (n q t)"),
-        )
 
-        vt_codes = [keep.tile([P, E], U32, name=f"vt_codes{n}", align_bytes=64) for n in range(2)]
-        vt_scales = [keep.tile([P, E], U8, name=f"vt_scales{n}", align_bytes=64) for n in range(2)]
-
-        def turn_and_quantise(listed, store, b):
-            pairs = listed[:].bitcast(F32)
+        def gather_and_turn(store, b, on_vector):
+            listed = sbuf(f"listed{store}{b}", [P, I], BF16)
+            gather(listed, (first_store, second_store)[store][b], (token_list, column_list)[store], on_vector)
+            pairs = listed.bitcast(F32)
             turned = turn.tile([P, 2, P], F32, name="turned")
             for u in range(2):
-                nc.tensor.transpose(turned[:, u, :], pairs[:, u : I // 2 : 2], identity[:])
-            vt = ring.tile([P, P, 2], F32, name="vt", align_bytes=64)
-            nc.scalar.copy(out=vt[:], in_=turned[:].rearrange("p u e -> p e u"))
-            cols = slice(b * P, (b + 1) * P)
-            nc.vector.quantize_mx(
-                out=vt_codes[store][:, cols].bitcast(FP8X4),
-                scales=vt_scales[store][:, cols],
-                in_=vt[:].rearrange("p e u -> p (e u)").bitcast(BF16),
-            )
+                nc.tensor.transpose(turned[:, u, :], pairs[:, u : I // 2 : 2], identity)
+            return turned[:]
 
-        def multiply_and_store(first, last):
-            cols = slice(first * P, last * P)
-            width = (last - first) * P
-            acc = psum.tile([P, width], F32, name=f"acc{first}")
-            for store in (1, 0):
-                rows = slice(store * Q, (store + 1) * Q)
-                nc.tensor.matmul_mx(
-                    out=acc[:],
-                    lhsT=wt_codes[:, rows].bitcast(FP8X4),
-                    lhsT_scale=wt_scales[:, rows],
-                    rhs=vt_codes[store][:, cols].bitcast(FP8X4),
-                    rhs_scale=vt_scales[store][:, cols],
-                    start=(store == 1),
-                    stop=(store == 0),
-                )
-            result = keep.tile([P, width], F32, name=f"result{first}")
-            nc.vector.tensor_copy(out=result[:], in_=acc[:])
-            nc.sync.dma_start(out=out[:, cols], in_=result[:])
+        def interleave(copy, vt, turned):
+            copy(out=vt.rearrange("p (e u) -> p e u", u=2), in_=turned.rearrange("p u e -> p e u"))
+
+        values = {}
+
+        def multiply_and_store(begin, end, result, copy):
+            acc = psum.tile([P, (end - begin) * P], F32, name=f"acc{begin}")
+            for b in range(begin, end):
+                block = acc[:, (b - begin) * P : (b - begin + 1) * P]
+                multiply(block, columns_of(weights, SECOND), values[SECOND, b], True, False)
+                multiply(block, columns_of(weights, FIRST), values[FIRST, b], False, True)
+            copy(out=result, in_=acc[:])
+            nc.sync.dma_start(out=out[:, begin * P : end * P], in_=result)
 
         for b in range(BLOCKS):
-            listed2 = ring.tile([P, I], BF16, name="listed2")
-            nc.vector.tensor_copy(listed2[:], val2_pool[b][:].indirect(list3[:]))
-            turn_and_quantise(listed2, 1, b)
-            listed1 = ring.tile([P, I], BF16, name="listed1")
-            if b < BLOCKS - 1:
-                nc.scalar.activation(listed1[:], val1_pool[b][:].indirect(list1[:]), ACT.Copy)
-            else:
-                half = LIST_COLS // 2
-                nc.vector.tensor_copy(listed1[:, : I // 2], val1_pool[b][:].indirect(list1[:, :half]))
-                nc.scalar.activation(listed1[:, I // 2 :], val1_pool[b][:].indirect(list1[:, half:]), ACT.Copy)
-            turn_and_quantise(listed1, 0, b)
-            if b == 1:
-                multiply_and_store(0, 2)
-            elif b > 1:
-                multiply_and_store(b, b + 1)
+            vt = sbuf(f"vt_second{b}", [P, 2 * P], F32)
+            interleave(nc.vector.tensor_copy, vt, gather_and_turn(SECOND, b, I))
+            values[SECOND, b] = quantise(f"vt_second{b}", vt.bitcast(BF16))
+        for j in range(2):
+            gather_notes(j, 0)
+        for j in range(2):
+            gather_keys(j, 0)
+        gather_notes(2, I)
+        larger(0)
+        gather_notes(3, I)
+        gather_keys(2, 0)
+        gather_keys(3, VECTOR_SHARE)
+        larger(1)
+
+        query_words = sbuf("query_words", [P, Q, PACK], BF16)
+        nc.scalar.copy(out=query_words, in_=query_rows.rearrange("p j q -> p q j"))
+        query_mx = quantise("query", query_words.rearrange("p q j -> p (q j)"))
+
+        zk = sbuf("zk", [P, I, 2], F32)
+        pair_words = zk_pairs.rearrange("p h i j -> p h (i j)").bitcast(F32)
+        nc.vector.tensor_copy(
+            out=zk.rearrange("p (t s) h -> p s t h", t=PACK),
+            in_=pair_words.rearrange("p h (s t) -> p s t h", t=PACK),
+        )
+        zk_mx = quantise("zk", zk.rearrange("p c h -> p (c h)").bitcast(BF16))
+        scores = psum.tile([P, PACK, Q], F32, name="scores")
+        for t in range(PACK):
+            multiply(scores[:, t, :], columns_of(zk_mx, t), query_mx, True, True)
+        w = sbuf("w", [P, Q, PACK], F32)
+        nc.scalar.activation(w, scores[:].rearrange("p t q -> p q t"), ACT.Sigmoid)
+
+        vt01 = sbuf("vt_first01", [P, 2, 2 * P], F32)
+        interleave(nc.scalar.copy, vt01[:, 0, :], gather_and_turn(FIRST, 0, 0))
+        turned1 = gather_and_turn(FIRST, 1, I)
+
+        wt = sbuf("wt", [P, 2, Q, PACK], BF16, buffer="first_store1")
+        for store in (FIRST, SECOND):
+            nc.vector.tensor_tensor(
+                out=wt[:, store],
+                in0=w,
+                in1=factors[store].unsqueeze(1).to_broadcast([P, Q, PACK]),
+                op=ALU.mult,
+            )
+        weights = quantise("wt", wt.rearrange("p n q t -> p (n q t)"))
+
+        interleave(nc.scalar.copy, vt01[:, 1, :], turned1)
+        values01 = quantise("vt_first01", vt01.rearrange("p b c -> p (b c)").bitcast(BF16))
+        for b in range(2):
+            values[FIRST, b] = columns_of(values01, b)
+
+        turned2 = gather_and_turn(FIRST, 2, 0)
+        turned3 = gather_and_turn(FIRST, 3, VECTOR_SHARE)
+
+        after_last = sbuf("after_last", [P, 2, 2 * P], F32, buffer="first_store3")
+        result01, vt2 = after_last[:, 0, :], after_last[:, 1, :]
+        multiply_and_store(0, 2, result01, nc.vector.tensor_copy)
+        interleave(nc.scalar.copy, vt2, turned2)
+        values[FIRST, 2] = quantise("vt_first2", vt2.bitcast(BF16))
+        vt3 = sbuf("vt_first3", [P, 2 * P], F32)
+        interleave(nc.scalar.copy, vt3, turned3)
+        values[FIRST, 3] = quantise("vt_first3", vt3.bitcast(BF16))
+        multiply_and_store(2, 3, sbuf("result2", [P, P], F32), nc.scalar.copy)
+        multiply_and_store(3, 4, sbuf("result3", [P, P], F32), nc.vector.tensor_copy)

@@ -19,6 +19,7 @@ P = 128
 PACK = 4
 BLOCKS = E // P
 SLOTS_PER_COLUMN = 16
+EARLY_BLOCKS = 3
 FIRST, SECOND = 0, 1
 VECTOR_SHARE = 288
 ALIGN = 64
@@ -56,14 +57,15 @@ def tile_attend_keylarger_twostores_lean_kernel(
         nc.sync.dma_start(column_list, offs3)
         nc.sync.dma_start(out=note_pairs[0], in_=note_rows[:, : 2 * U])
         nc.sync.dma_start(note_list, offs2)
-        for b in range(1, BLOCKS):
-            nc.scalar.dma_start(out=second_store[b], in_=vals2[b * P : (b + 1) * P, :])
+        for b in range(1, EARLY_BLOCKS):
+            nc.sync.dma_start(out=second_store[b], in_=vals2[b * P : (b + 1) * P, :])
         nc.sync.dma_start(out=key_planes01, in_=key_rows[:, : 2 * T])
         nc.sync.dma_start(token_list, offs)
         nc.sync.dma_start(out=note_pairs[1], in_=note_rows[:, 2 * U :])
         nc.sync.dma_start(out=key_plane2, in_=key_rows[:, 2 * T : 3 * T])
         nc.sync.dma_start(out=key_plane3, in_=key_rows[:, 3 * T :])
         nc.sync.dma_start(out=query_rows, in_=query.rearrange("(p j) q -> p j q", j=PACK))
+        nc.sync.dma_start(out=second_store[3], in_=vals2[3 * P :, :])
         for b in range(BLOCKS):
             nc.sync.dma_start(out=first_store[b], in_=vals[b * P : (b + 1) * P, :])
         for factor, row in zip(factors, (factor1, factor2)):
@@ -79,9 +81,9 @@ def tile_attend_keylarger_twostores_lean_kernel(
             if on_vector < I:
                 nc.scalar.activation(listed[:, on_vector:], window.indirect(offsets[:, cut:]), ACT.Copy)
 
-        def quantise(name, words):
+        def quantise(name, words, buffer=None):
             columns = words.shape[1] // PACK
-            codes = sbuf(f"{name}_codes", [P, columns], U32)
+            codes = sbuf(f"{name}_codes", [P, columns], U32, buffer)
             scales = sbuf(f"{name}_scales", [P, columns], U8)
             nc.vector.quantize_mx(out=codes.bitcast(FP8X4), scales=scales, in_=words)
             return codes, scales
@@ -141,7 +143,7 @@ def tile_attend_keylarger_twostores_lean_kernel(
             copy(out=result, in_=acc[:])
             nc.sync.dma_start(out=out[:, begin * P : end * P], in_=result)
 
-        for b in range(BLOCKS):
+        for b in range(EARLY_BLOCKS):
             vt = sbuf(f"vt_second{b}", [P, 2 * P], F32)
             interleave(nc.vector.tensor_copy, vt, gather_and_turn(SECOND, b, I))
             values[SECOND, b] = quantise(f"vt_second{b}", vt.bitcast(BF16))
@@ -173,26 +175,31 @@ def tile_attend_keylarger_twostores_lean_kernel(
         w = sbuf("w", [P, Q, PACK], F32)
         nc.scalar.activation(w, scores[:].rearrange("p t q -> p q t"), ACT.Sigmoid)
 
-        vt01 = sbuf("vt_first01", [P, 2, 2 * P], F32)
-        interleave(nc.scalar.copy, vt01[:, 0, :], gather_and_turn(FIRST, 0, 0))
-        turned1 = gather_and_turn(FIRST, 1, I)
+        turned_second3 = gather_and_turn(SECOND, 3, 0)
+        turned0 = gather_and_turn(FIRST, 0, I)
 
-        wt = sbuf("wt", [P, 2, Q, PACK], BF16, buffer="first_store1")
+        behind0 = sbuf("behind0", [P, 3, Q * PACK], BF16, buffer="first_store0")
         for store in (FIRST, SECOND):
             nc.vector.tensor_tensor(
-                out=wt[:, store],
+                out=behind0[:, store, :].rearrange("p (q t) -> p q t", t=PACK),
                 in0=w,
                 in1=factors[store].unsqueeze(1).to_broadcast([P, Q, PACK]),
                 op=ALU.mult,
             )
-        weights = quantise("wt", wt.rearrange("p n q t -> p (n q t)"))
+        interleave(nc.scalar.copy, behind0[:, 2, :].bitcast(F32), turned_second3)
+        weights = quantise("behind0", behind0.rearrange("p n c -> p (n c)"))
+        values[SECOND, 3] = columns_of(weights, 2)
 
+        turned1 = gather_and_turn(FIRST, 1, 0)
+        vt01 = sbuf("vt_first01", [P, 2, 2 * P], F32, buffer="first_store1")
+        interleave(nc.scalar.copy, vt01[:, 0, :], turned0)
         interleave(nc.scalar.copy, vt01[:, 1, :], turned1)
-        values01 = quantise("vt_first01", vt01.rearrange("p b c -> p (b c)").bitcast(BF16))
+
+        turned2 = gather_and_turn(FIRST, 2, I)
+        values01 = quantise("vt_first01", vt01.rearrange("p b c -> p (b c)").bitcast(BF16), "first_store2")
         for b in range(2):
             values[FIRST, b] = columns_of(values01, b)
 
-        turned2 = gather_and_turn(FIRST, 2, 0)
         turned3 = gather_and_turn(FIRST, 3, VECTOR_SHARE)
 
         after_last = sbuf("after_last", [P, 2, 2 * P], F32, buffer="first_store3")

from contextlib import ExitStack

import concourse.mybir as mybir
from concourse.masks import make_identity

D, T, I, Q, E, U, X = 512, 2048, 512, 128, 512, 1024, 1024
FLOPS = 2 * Q * I * D + 2 * 2 * Q * I * E

F32 = mybir.dt.float32
BF16 = mybir.dt.bfloat16
U32 = mybir.dt.uint32
U16 = mybir.dt.uint16
U8 = mybir.dt.uint8
FP8X4 = mybir.dt.float8_e4m3fn_x4
ALU = mybir.AluOpType
ACT = mybir.ActivationFunctionType

P = 128
PACK = 4
BLOCKS = E // P
SLOTS_PER_COLUMN = 16
EARLY_BLOCKS = 3
FIRST, SECOND = 0, 1
VECTOR_SHARE = 288
ALIGN = 64


def tile_attend_keylarger_twostores_lean_kernel(
    tc, query, keys, notes, factor1, factor2, vals, vals2, offs, offs2, offs3, out
):
    nc = tc.nc
    with ExitStack() as ctx:
        keep = ctx.enter_context(tc.tile_pool(name="keep", bufs=1))
        psum = ctx.enter_context(tc.psum_pool(name="psum", bufs=1))
        turn = ctx.enter_context(tc.psum_pool(name="turn", bufs=4))

        def sbuf(name, shape, dtype, buffer=None):
            return keep.tile(shape, dtype, name=name, tag=buffer or name, align_bytes=ALIGN)[:]

        token_list = sbuf("token_list", [P, I // SLOTS_PER_COLUMN], U16)
        note_list = sbuf("note_list", [P, I // SLOTS_PER_COLUMN], U16)
        column_list = sbuf("column_list", [P, I // SLOTS_PER_COLUMN], U16)
        key_planes01 = sbuf("key_planes01", [P, 2 * T], F32)
        key_plane2 = sbuf("key_plane2", [P, T], F32)
        key_plane3 = sbuf("key_plane3", [P, T], F32)
        key_planes = [key_planes01[:, :T], key_planes01[:, T:], key_plane2, key_plane3]
        note_pairs = [sbuf(f"note_pair{h}", [P, 2 * U], F32) for h in range(2)]
        note_planes = [note_pairs[j // 2][:, (j % 2) * U : (j % 2 + 1) * U] for j in range(PACK)]
        first_store = [sbuf(f"first_store{b}", [P, T], F32) for b in range(BLOCKS)]
        second_store = [sbuf(f"second_store{b}", [P, X], F32) for b in range(BLOCKS)]
        query_rows = sbuf("query_rows", [P, PACK, Q], F32)
        factors = [sbuf(f"factor{store}", [P, PACK], F32) for store in (FIRST, SECOND)]

        key_rows = keys.rearrange("(p j) t -> p (j t)", j=PACK)
        note_rows = notes.rearrange("(p j) u -> p (j u)", j=PACK)
        nc.sync.dma_start(out=second_store[0], in_=vals2[:P, :])
        nc.sync.dma_start(column_list, offs3)
        nc.sync.dma_start(out=note_pairs[0], in_=note_rows[:, : 2 * U])
        nc.sync.dma_start(note_list, offs2)
        for b in range(1, EARLY_BLOCKS):
            nc.sync.dma_start(out=second_store[b], in_=vals2[b * P : (b + 1) * P, :])
        nc.sync.dma_start(out=key_planes01, in_=key_rows[:, : 2 * T])
        nc.sync.dma_start(token_list, offs)
        nc.sync.dma_start(out=note_pairs[1], in_=note_rows[:, 2 * U :])
        nc.sync.dma_start(out=key_plane2, in_=key_rows[:, 2 * T : 3 * T])
        nc.sync.dma_start(out=key_plane3, in_=key_rows[:, 3 * T :])
        nc.sync.dma_start(out=query_rows, in_=query.rearrange("(p j) q -> p j q", j=PACK))
        nc.sync.dma_start(out=second_store[3], in_=vals2[3 * P :, :])
        for b in range(BLOCKS):
            nc.sync.dma_start(out=first_store[b], in_=vals[b * P : (b + 1) * P, :])
        for factor, row in zip(factors, (factor1, factor2)):
            nc.gpsimd.dma_start(out=factor, in_=row.rearrange("o (p t) -> (o p) t", t=PACK))

        identity = sbuf("identity", [P, P], F32)
        make_identity(nc, identity)

        def gather(listed, window, offsets, on_vector):
            cut = on_vector // SLOTS_PER_COLUMN
            if on_vector > 0:
                nc.vector.tensor_copy(listed[:, :on_vector], window.indirect(offsets[:, :cut]))
            if on_vector < I:
                nc.scalar.activation(listed[:, on_vector:], window.indirect(offsets[:, cut:]), ACT.Copy)

        def quantise(name, words, buffer=None):
            columns = words.shape[1] // PACK
            codes = sbuf(f"{name}_codes", [P, columns], U32, buffer)
            scales = sbuf(f"{name}_scales", [P, columns], U8)
            nc.vector.quantize_mx(out=codes.bitcast(FP8X4), scales=scales, in_=words)
            return codes, scales

        def columns_of(quantised, n):
            return [part[:, n * P : (n + 1) * P] for part in quantised]

        def multiply(acc, stationary, moving, start, stop):
            nc.tensor.matmul_mx(
                out=acc,
                lhsT=stationary[0].bitcast(FP8X4),
                lhsT_scale=stationary[1],
                rhs=moving[0].bitcast(FP8X4),
                rhs_scale=moving[1],
                start=start,
                stop=stop,
            )

        keys_listed = [sbuf(f"keys_listed{h}", [P, 2, I], F32) for h in range(2)]
        notes_listed = [sbuf(f"notes_listed{h}", [P, 2, I], F32) for h in range(2)]
        zk_pairs = sbuf("zk_pairs", [P, 2, I, 2], BF16)

        def gather_keys(j, on_vector):
            gather(keys_listed[j // 2][:, j % 2, :], key_planes[j], token_list, on_vector)

        def gather_notes(j, on_vector):
            gather(notes_listed[j // 2][:, j % 2, :], note_planes[j], note_list, on_vector)

        def larger(h):
            nc.vector.tensor_tensor(
                out=zk_pairs[:, h],
                in0=keys_listed[h].rearrange("p j i -> p i j"),
                in1=notes_listed[h].rearrange("p j i -> p i j"),
                op=ALU.max,
            )

        def gather_and_turn(store, b, on_vector):
            listed = sbuf(f"listed{store}{b}", [P, I], BF16)
            gather(listed, (first_store, second_store)[store][b], (token_list, column_list)[store], on_vector)
            pairs = listed.bitcast(F32)
            turned = turn.tile([P, 2, P], F32, name="turned")
            for u in range(2):
                nc.tensor.transpose(turned[:, u, :], pairs[:, u : I // 2 : 2], identity)
            return turned[:]

        def interleave(copy, vt, turned):
            copy(out=vt.rearrange("p (e u) -> p e u", u=2), in_=turned.rearrange("p u e -> p e u"))

        values = {}

        def multiply_and_store(begin, end, result, copy):
            acc = psum.tile([P, (end - begin) * P], F32, name=f"acc{begin}")
            for b in range(begin, end):
                block = acc[:, (b - begin) * P : (b - begin + 1) * P]
                multiply(block, columns_of(weights, SECOND), values[SECOND, b], True, False)
                multiply(block, columns_of(weights, FIRST), values[FIRST, b], False, True)
            copy(out=result, in_=acc[:])
            nc.sync.dma_start(out=out[:, begin * P : end * P], in_=result)

        for b in range(EARLY_BLOCKS):
            vt = sbuf(f"vt_second{b}", [P, 2 * P], F32)
            interleave(nc.vector.tensor_copy, vt, gather_and_turn(SECOND, b, I))
            values[SECOND, b] = quantise(f"vt_second{b}", vt.bitcast(BF16))
        for j in range(2):
            gather_notes(j, 0)
        for j in range(2):
            gather_keys(j, 0)
        gather_notes(2, I)
        larger(0)
        gather_notes(3, I)
        gather_keys(2, 0)
        gather_keys(3, VECTOR_SHARE)
        larger(1)

        query_words = sbuf("query_words", [P, Q, PACK], BF16)
        nc.scalar.copy(out=query_words, in_=query_rows.rearrange("p j q -> p q j"))
        query_mx = quantise("query", query_words.rearrange("p q j -> p (q j)"))

        zk = sbuf("zk", [P, I, 2], F32)
        pair_words = zk_pairs.rearrange("p h i j -> p h (i j)").bitcast(F32)
        nc.vector.tensor_copy(
            out=zk.rearrange("p (t s) h -> p s t h", t=PACK),
            in_=pair_words.rearrange("p h (s t) -> p s t h", t=PACK),
        )
        zk_mx = quantise("zk", zk.rearrange("p c h -> p (c h)").bitcast(BF16))
        scores = psum.tile([P, PACK, Q], F32, name="scores")
        for t in range(PACK):
            multiply(scores[:, t, :], columns_of(zk_mx, t), query_mx, True, True)
        w = sbuf("w", [P, Q, PACK], F32)
        nc.scalar.activation(w, scores[:].rearrange("p t q -> p q t"), ACT.Sigmoid)

        turned_second3 = gather_and_turn(SECOND, 3, 0)
        turned0 = gather_and_turn(FIRST, 0, I)

        behind0 = sbuf("behind0", [P, 3, Q * PACK], BF16, buffer="first_store0")
        for store in (FIRST, SECOND):
            nc.vector.tensor_tensor(
                out=behind0[:, store, :].rearrange("p (q t) -> p q t", t=PACK),
                in0=w,
                in1=factors[store].unsqueeze(1).to_broadcast([P, Q, PACK]),
                op=ALU.mult,
            )
        interleave(nc.scalar.copy, behind0[:, 2, :].bitcast(F32), turned_second3)
        weights = quantise("behind0", behind0.rearrange("p n c -> p (n c)"))
        values[SECOND, 3] = columns_of(weights, 2)

        turned1 = gather_and_turn(FIRST, 1, 0)
        vt01 = sbuf("vt_first01", [P, 2, 2 * P], F32, buffer="first_store1")
        interleave(nc.scalar.copy, vt01[:, 0, :], turned0)
        interleave(nc.scalar.copy, vt01[:, 1, :], turned1)

        turned2 = gather_and_turn(FIRST, 2, I)
        values01 = quantise("vt_first01", vt01.rearrange("p b c -> p (b c)").bitcast(BF16), "first_store2")
        for b in range(2):
            values[FIRST, b] = columns_of(values01, b)

        turned3 = gather_and_turn(FIRST, 3, VECTOR_SHARE)

        after_last = sbuf("after_last", [P, 2, 2 * P], F32, buffer="first_store3")
        result01, vt2 = after_last[:, 0, :], after_last[:, 1, :]
        multiply_and_store(0, 2, result01, nc.vector.tensor_copy)
        interleave(nc.scalar.copy, vt2, turned2)
        values[FIRST, 2] = quantise("vt_first2", vt2.bitcast(BF16))
        vt3 = sbuf("vt_first3", [P, 2 * P], F32)
        interleave(nc.scalar.copy, vt3, turned3)
        values[FIRST, 3] = quantise("vt_first3", vt3.bitcast(BF16))
        multiply_and_store(2, 3, sbuf("result2", [P, P], F32), nc.scalar.copy)
        multiply_and_store(3, 4, sbuf("result3", [P, P], F32), nc.vector.tensor_copy)
